import numpy as np
import ml_dtypes


def mxq(x, axis, fmt="e4m3"):
    dtype, down = {"e4m3": (ml_dtypes.float8_e4m3fn, 7), "e5m2": (ml_dtypes.float8_e5m2, 14)}[fmt]
    v = np.moveaxis(np.asarray(x, np.float32).astype(ml_dtypes.bfloat16).astype(np.float64), axis, -1)
    blocks = v.reshape(v.shape[:-1] + (-1, 32))
    amax = np.abs(blocks).max(-1, keepdims=True)
    byte = np.maximum(np.where(amax > 0, np.frexp(amax)[1] - 1 + 127, 0) - down, 1)
    scale = np.exp2(byte - 127.0)
    codes = (blocks / scale).astype(np.float32).astype(dtype).astype(np.float64)
    return np.moveaxis((codes * scale).reshape(v.shape), -1, axis)


WIDE = False


def mx_kscale(k):
    if not WIDE:
        return np.ones(k)
    levels = np.array([10, -10, 5, -5, 0])
    if k % 512:
        return np.exp2(np.random.permutation(np.resize(levels, k // 32))).repeat(32)
    a = np.empty((k // 512, 16))
    for p in range(k // 512):
        a[p, :8] = np.random.permutation(np.resize(levels, 8))
        for g in range(8):
            far = levels[np.abs(levels - a[p, g]) >= 10]
            a[p, g + 8] = far[np.random.randint(len(far))]
    return np.exp2(a.ravel()).repeat(32)


def f64(x):
    return np.asarray(x).astype(np.float64)


def striped(idx):
    return np.tile(idx.reshape(-1, 16).T, (8, 1)).astype(np.uint16)


def unstriped(offs):
    return offs[:16].T.reshape(-1).astype(np.int64)


def pack_weight(w):
    k, n = w.shape
    w = f64(np.asarray(w, np.float32).astype(ml_dtypes.bfloat16)).reshape(k // 32, 32, n)
    amax = np.abs(w).max(1)
    byte = np.clip(np.where(amax > 0, np.frexp(amax)[1] - 1 + 127 - 7, 1), 1, 254)
    scaled = (w * np.exp2(127.0 - byte)[:, None, :]).reshape(k, n).astype(np.float32)
    words = np.ascontiguousarray(scaled.reshape(k // 512, 128, 4, n).transpose(0, 1, 3, 2)).astype(ml_dtypes.float8_e4m3fn).view(np.uint8)
    return words, np.ascontiguousarray(byte.astype(np.uint8).reshape(k // 512, 16, n))


def unpack_weight(words, scales):
    g, p, n, _ = words.shape
    vals = np.ascontiguousarray(words).view(ml_dtypes.float8_e4m3fn).astype(np.float64) * np.repeat(np.exp2(scales.astype(np.float64) - 127.0), 8, axis=1)[..., None]
    return vals.transpose(0, 1, 3, 2).reshape(g * 512, n)


def relu(v):
    return np.maximum(v, 0.0)


K, T, S, N, U = 512, 2048, 1024, 128, 2048


def setup_inputs():
    n = np.random.standard_normal
    s = mx_kscale(K)[:, None]
    packed_w1 = pack_weight(n((K, N)) / np.sqrt(K) / s)
    return {
        "xT": (n((K, T)) * s).astype(np.float32),
        "w1_words": packed_w1[0],
        "w1_scales": packed_w1[1],
        "res": n((N, U)).astype(np.float32),
        "offs": striped(np.random.permutation(T)[:S]),
        "own": striped(np.random.randint(0, S, U)),
    }


def reference(xT, w1_words, w1_scales, res, offs, own):
    xq = mxq(f64(xT)[:, unstriped(offs)], 0, "e4m3")
    y = relu(unpack_weight(w1_words, w1_scales).T @ xq)
    return f64(res) + y[:, unstriped(own)]

@@ -1,0 +1,125 @@
+from contextlib import ExitStack
+
+import concourse.mybir as mybir
+
+K, T, S, M, U = 512, 2048, 1024, 128, 2048
+FLOPS = 2 * K * M * S
+
+F32 = mybir.dt.float32
+BF16 = mybir.dt.bfloat16
+I32 = mybir.dt.int32
+U32 = mybir.dt.uint32
+U16 = mybir.dt.uint16
+U8 = mybir.dt.uint8
+FP8X4 = mybir.dt.float8_e4m3fn_x4
+COPY = mybir.ActivationFunctionType.Copy
+RELU = mybir.ActivationFunctionType.Relu
+ADD = mybir.AluOpType.add
+
+P = 128
+LIST_ROWS = 16
+PICK = 256
+LOADS = (
+    ((1024, 384), (1024, 384)),
+    ((1024, 768), (512, 0), (256, 0), (256, 0)),
+)
+OUT_WIDTHS = (768, 768, 384, 128)
+
+
+def tile_picked_unmerge_relu_e_kernel(tc, xT, w1_words, w1_scales, res, offs, own, out):
+    nc = tc.nc
+    rows = xT.rearrange("(p j) t -> p j t", j=4)
+    with ExitStack() as ctx:
+        keep = ctx.enter_context(tc.tile_pool(name="keep", bufs=1))
+        psum = ctx.enter_context(tc.psum_pool(name="psum", bufs=1))
+
+        picks = keep.tile([P, S // LIST_ROWS], U16, name="picks")
+        owners = keep.tile([P, U // LIST_ROWS], U16, name="owners")
+        w_words = keep.tile([P, M], U32, name="w_words", align_bytes=64)
+        w_scales = keep.tile([P, M], U8, name="w_scales", align_bytes=64)
+        res_sb = keep.tile([P, U], F32, name="res_sb")
+        y = keep.tile([P, S], F32, name="y")
+
+        nc.vector.memset(w_scales[:].bitcast(I32), 0)
+
+        raws = []
+        for u, chunks in enumerate(LOADS):
+            start = 0
+            for width, engine in chunks:
+                raw = keep.tile([P, 2, width], F32, name=f"raw{u}_{start}")
+                nc.sync.dma_start(out=raw[:], in_=rows[:, 2 * u : 2 * u + 2, start : start + width])
+                if not raws:
+                    nc.sync.dma_start(picks[:], offs)
+                raws.append((u, start, width, engine, raw))
+                start += width
+        nc.sync.dma_start(out=w_words[:].bitcast(I32), in_=w1_words[0].rearrange("p n t -> p (n t)").bitcast(I32))
+        for q in range(4):
+            nc.sync.dma_start(out=w_scales[32 * q : 32 * q + 4, :].bitcast(I32), in_=w1_scales[0, 4 * q : 4 * q + 4, :].bitcast(I32))
+        nc.sync.dma_start(owners[:], own)
+        nc.sync.dma_start(out=res_sb[:], in_=res)
+
+        pairs = [keep.tile([P, 2 * T], BF16, name=f"pairs{u}", align_bytes=64) for u in range(2)]
+        n_picks = S // PICK
+        last = n_picks - 1
+        halves = keep.tile([P, 2 * S], U32, name="halves", align_bytes=64)
+        woven = [keep.tile([P, 4 * PICK], BF16, name=f"woven{c}", align_bytes=64) for c in range(n_picks)]
+        codes = [keep.tile([P, PICK], U32, name=f"codes{c}", align_bytes=64) for c in range(n_picks)]
+        scales = [keep.tile([P, PICK], U8, name=f"scales{c}", align_bytes=64) for c in range(n_picks)]
+        banks = [psum.tile([P, PICK], F32, name=f"bank{c}") for c in range(n_picks)]
+
+        def round_pairs(u):
+            for v, start, width, on_scalar, raw in raws:
+                if v == u:
+                    dst = pairs[u][:, 2 * start : 2 * (start + width)].rearrange("p (c e) -> p c e", e=2)
+                    src = raw[:].rearrange("p e c -> p c e")
+                    if on_scalar:
+                        nc.scalar.activation(out=dst[:, :on_scalar, :], in_=src[:, :on_scalar, :], func=COPY)
+                    nc.vector.tensor_copy(out=dst[:, on_scalar:, :], in_=src[:, on_scalar:, :])
+
+        def woven_words(c):
+            return woven[c][:].bitcast(U32).rearrange("p (n u) -> p n u", u=2)
+
+        def gather(u, start, width):
+            window = pairs[u][:].bitcast(U32).indirect(picks[:, start // LIST_ROWS : (start + width) // LIST_ROWS])
+            nc.vector.tensor_copy(out=halves[:, u * S + start : u * S + start + width], in_=window)
+
+        def weave(c):
+            src = halves[:].rearrange("p (u n) -> p n u", u=2)
+            nc.scalar.copy(out=woven_words(c), in_=src[:, c * PICK : (c + 1) * PICK, :])
+
+        def multiply(c):
+            nc.vector.quantize_mx(out=codes[c][:].bitcast(FP8X4), scales=scales[c][:], in_=woven[c][:])
+            nc.tensor.matmul_mx(
+                out=banks[c][:],
+                lhsT=w_words[:].bitcast(FP8X4),
+                lhsT_scale=w_scales[:],
+                rhs=codes[c][:].bitcast(FP8X4),
+                rhs_scale=scales[c][:],
+                start=True,
+                stop=True,
+            )
+
+        def rectify(c):
+            dst = y[:, c * PICK : (c + 1) * PICK]
+            if c == last:
+                nc.vector.tensor_scalar_max(out=dst, in0=banks[c][:], scalar1=0.0)
+            else:
+                nc.scalar.activation(out=dst, in_=banks[c][:], func=RELU)
+
+        round_pairs(0)
+        gather(0, 0, S)
+        round_pairs(1)
+        for c in range(n_picks):
+            gather(1, c * PICK, PICK)
+            weave(c)
+        for c in range(n_picks):
+            multiply(c)
+            rectify(c)
+
+        start = 0
+        for width in OUT_WIDTHS:
+            summed = keep.tile([P, width], F32, name=f"summed{start}")
+            window = y[:].indirect(owners[:, start // LIST_ROWS : (start + width) // LIST_ROWS])
+            nc.vector.tensor_tensor(out=summed[:], in0=window, in1=res_sb[:, start : start + width], op=ADD)
+            nc.sync.dma_start(out=out[:, start : start + width], in_=summed[:])
+            start += width

@@ -19,10 +19,9 @@ ADD = mybir.AluOpType.add
 P = 128
 LIST_ROWS = 16
 PICK = 256
-LOADS = (
-    ((1024, 384), (1024, 384)),
-    ((1024, 768), (512, 0), (256, 0), (256, 0)),
-)
+PLANE2_LOADS = ((1024, 256), (1024, 256))
+PAIR_LOADS = ((1024, 0), (768, 256), (256, 64))
+PLANE3_LOADS = ((512, 512), (512, 512), (512, 512), (512, 512))
 OUT_WIDTHS = (768, 768, 384, 128)
 
 
@@ -42,79 +41,103 @@ def tile_picked_unmerge_relu_e_kernel(tc, xT, w1_words, w1_scales, res, offs, ow
 
         nc.vector.memset(w_scales[:].bitcast(I32), 0)
 
-        raws = []
-        for u, chunks in enumerate(LOADS):
+        planes = {j: keep.tile([P, T], F32, name=f"plane{j}") for j in (2, 3)}
+        rounded = {j: keep.tile([P, T], BF16, name=f"rounded{j}") for j in (2, 3)}
+
+        def spans(chunks):
             start = 0
-            for width, engine in chunks:
-                raw = keep.tile([P, 2, width], F32, name=f"raw{u}_{start}")
-                nc.sync.dma_start(out=raw[:], in_=rows[:, 2 * u : 2 * u + 2, start : start + width])
-                if not raws:
-                    nc.sync.dma_start(picks[:], offs)
-                raws.append((u, start, width, engine, raw))
+            found = []
+            for width, on_scalar in chunks:
+                found.append((start, width, on_scalar))
                 start += width
+            return found
+
+        def load_plane(j, chunks):
+            for start, width, on_scalar in spans(chunks):
+                nc.sync.dma_start(out=planes[j][:, start : start + width], in_=rows[:, j, start : start + width])
+
+        load_plane(2, PLANE2_LOADS)
+        nc.sync.dma_start(picks[:], offs)
+        raws = []
+        for start, width, on_scalar in spans(PAIR_LOADS):
+            raw = keep.tile([P, 2, width], F32, name=f"raw{start}")
+            nc.sync.dma_start(out=raw[:], in_=rows[:, 0:2, start : start + width])
+            raws.append(raw)
+        load_plane(3, PLANE3_LOADS)
         nc.sync.dma_start(out=w_words[:].bitcast(I32), in_=w1_words[0].rearrange("p n t -> p (n t)").bitcast(I32))
         for q in range(4):
             nc.sync.dma_start(out=w_scales[32 * q : 32 * q + 4, :].bitcast(I32), in_=w1_scales[0, 4 * q : 4 * q + 4, :].bitcast(I32))
         nc.sync.dma_start(owners[:], own)
         nc.sync.dma_start(out=res_sb[:], in_=res)
 
-        pairs = [keep.tile([P, 2 * T], BF16, name=f"pairs{u}", align_bytes=64) for u in range(2)]
+        pairs = keep.tile([P, 2 * T], BF16, name="pairs", align_bytes=64)
         n_picks = S // PICK
         last = n_picks - 1
-        halves = keep.tile([P, 2 * S], U32, name="halves", align_bytes=64)
         woven = [keep.tile([P, 4 * PICK], BF16, name=f"woven{c}", align_bytes=64) for c in range(n_picks)]
-        codes = [keep.tile([P, PICK], U32, name=f"codes{c}", align_bytes=64) for c in range(n_picks)]
-        scales = [keep.tile([P, PICK], U8, name=f"scales{c}", align_bytes=64) for c in range(n_picks)]
-        banks = [psum.tile([P, PICK], F32, name=f"bank{c}") for c in range(n_picks)]
+        blocks = [(c, 0, PICK) for c in range(last)] + [(last, 0, PICK // 2), (last, PICK // 2, PICK // 2)]
 
-        def round_pairs(u):
-            for v, start, width, on_scalar, raw in raws:
-                if v == u:
-                    dst = pairs[u][:, 2 * start : 2 * (start + width)].rearrange("p (c e) -> p c e", e=2)
-                    src = raw[:].rearrange("p e c -> p c e")
-                    if on_scalar:
-                        nc.scalar.activation(out=dst[:, :on_scalar, :], in_=src[:, :on_scalar, :], func=COPY)
-                    nc.vector.tensor_copy(out=dst[:, on_scalar:, :], in_=src[:, on_scalar:, :])
+        def shared_round(dst, src, width, on_scalar):
+            if on_scalar > 0:
+                nc.scalar.activation(out=dst[:, :on_scalar], in_=src[:, :on_scalar], func=COPY)
+            if on_scalar < width:
+                nc.vector.tensor_copy(out=dst[:, on_scalar:], in_=src[:, on_scalar:])
 
-        def woven_words(c):
-            return woven[c][:].bitcast(U32).rearrange("p (n u) -> p n u", u=2)
+        def round_plane(j, chunks):
+            for start, width, on_scalar in spans(chunks):
+                shared_round(rounded[j][:, start : start + width], planes[j][:, start : start + width], width, on_scalar)
 
-        def gather(u, start, width):
-            window = pairs[u][:].bitcast(U32).indirect(picks[:, start // LIST_ROWS : (start + width) // LIST_ROWS])
-            nc.vector.tensor_copy(out=halves[:, u * S + start : u * S + start + width], in_=window)
+        def round_pairs():
+            for (start, width, on_scalar), raw in zip(spans(PAIR_LOADS), raws):
+                dst = pairs[:, 2 * start : 2 * (start + width)].rearrange("p (c e) -> p c e", e=2)
+                shared_round(dst, raw[:].rearrange("p e c -> p c e"), width, on_scalar)
 
-        def weave(c):
-            src = halves[:].rearrange("p (u n) -> p n u", u=2)
-            nc.scalar.copy(out=woven_words(c), in_=src[:, c * PICK : (c + 1) * PICK, :])
+        def entries(c):
+            cols = PICK // LIST_ROWS
+            return picks[:, c * cols : (c + 1) * cols]
 
-        def multiply(c):
-            nc.vector.quantize_mx(out=codes[c][:].bitcast(FP8X4), scales=scales[c][:], in_=woven[c][:])
+        def gather_plane(j, c):
+            dst = woven[c][:].rearrange("p (n t) -> p n t", t=4)[:, :, j]
+            if c == 0:
+                nc.vector.tensor_copy(out=dst, in_=planes[j][:].indirect(entries(c)))
+            else:
+                nc.scalar.activation(out=dst, in_=rounded[j][:].indirect(entries(c)), func=COPY)
+
+        def gather_pairs(c):
+            dst = woven[c][:].bitcast(U32).rearrange("p (n u) -> p n u", u=2)[:, :, 0]
+            nc.vector.tensor_copy(out=dst, in_=pairs[:].bitcast(U32).indirect(entries(c)))
+
+        def multiply(b):
+            c, start, width = blocks[b]
+            codes = keep.tile([P, width], U32, name=f"codes{b}", align_bytes=64)
+            scales = keep.tile([P, width], U8, name=f"scales{b}", align_bytes=64)
+            bank = psum.tile([P, width], F32, name=f"bank{b}")
+            nc.vector.quantize_mx(out=codes[:].bitcast(FP8X4), scales=scales[:], in_=woven[c][:, 4 * start : 4 * (start + width)])
             nc.tensor.matmul_mx(
-                out=banks[c][:],
+                out=bank[:],
                 lhsT=w_words[:].bitcast(FP8X4),
                 lhsT_scale=w_scales[:],
-                rhs=codes[c][:].bitcast(FP8X4),
-                rhs_scale=scales[c][:],
+                rhs=codes[:].bitcast(FP8X4),
+                rhs_scale=scales[:],
                 start=True,
                 stop=True,
             )
-
-        def rectify(c):
-            dst = y[:, c * PICK : (c + 1) * PICK]
-            if c == last:
-                nc.vector.tensor_scalar_max(out=dst, in0=banks[c][:], scalar1=0.0)
+            dst = y[:, c * PICK + start : c * PICK + start + width]
+            if b == len(blocks) - 1:
+                nc.vector.tensor_scalar_max(out=dst, in0=bank[:], scalar1=0.0)
             else:
-                nc.scalar.activation(out=dst, in_=banks[c][:], func=RELU)
+                nc.scalar.activation(out=dst, in_=bank[:], func=RELU)
 
-        round_pairs(0)
-        gather(0, 0, S)
-        round_pairs(1)
+        round_plane(2, PLANE2_LOADS)
         for c in range(n_picks):
-            gather(1, c * PICK, PICK)
-            weave(c)
+            gather_plane(2, c)
+        round_pairs()
+        for c in list(range(1, n_picks)) + [0]:
+            gather_pairs(c)
+        round_plane(3, PLANE3_LOADS)
         for c in range(n_picks):
-            multiply(c)
-            rectify(c)
+            gather_plane(3, c)
+        for b in range(len(blocks)):
+            multiply(b)
 
         start = 0
         for width in OUT_WIDTHS:

@@ -18,11 +18,15 @@ ADD = mybir.AluOpType.add
 
 P = 128
 LIST_ROWS = 16
-PICK = 256
-PLANE2_LOADS = ((1024, 256), (1024, 256))
-PAIR_LOADS = ((1024, 0), (768, 256), (256, 64))
-PLANE3_LOADS = ((512, 512), (512, 512), (512, 512), (512, 512))
-OUT_WIDTHS = (768, 768, 384, 128)
+PLANES = (
+    (2, 384, ((1024, 384), (1024, 384))),
+    (0, 352, ((1024, 0), (1024, 0))),
+    (1, 352, ((1024, 0), (512, 0), (512, 0))),
+    (3, 384, ((1024, 0), (768, 0), (256, 0))),
+)
+LAST_CUT = 768
+BANKS = (((0, 256), (256, 128)), ((384, 256), (640, 128)), ((768, 128),), ((896, 128),))
+OUT_WIDTHS = (864, 576, 320, 192, 96)
 
 
 def tile_picked_unmerge_relu_e_kernel(tc, xT, w1_words, w1_scales, res, offs, own, out):
@@ -39,10 +43,9 @@ def tile_picked_unmerge_relu_e_kernel(tc, xT, w1_words, w1_scales, res, offs, ow
         res_sb = keep.tile([P, U], F32, name="res_sb")
         y = keep.tile([P, S], F32, name="y")
 
-        nc.vector.memset(w_scales[:].bitcast(I32), 0)
-
-        planes = {j: keep.tile([P, T], F32, name=f"plane{j}") for j in (2, 3)}
-        rounded = {j: keep.tile([P, T], BF16, name=f"rounded{j}") for j in (2, 3)}
+        planes = [keep.tile([P, T], F32, name=f"plane{j}") for j in range(4)]
+        rounded = [keep.tile([P, T], BF16, name=f"rounded{j}") for j in range(4)]
+        woven = keep.tile([P, 4 * S], BF16, name="woven", align_bytes=64)
 
         def spans(chunks):
             start = 0
@@ -52,92 +55,59 @@ def tile_picked_unmerge_relu_e_kernel(tc, xT, w1_words, w1_scales, res, offs, ow
                 start += width
             return found
 
-        def load_plane(j, chunks):
+        nc.vector.memset(w_scales[:].bitcast(I32), 0)
+        for q in range(4):
+            nc.scalar.dma_start(out=w_scales[32 * q : 32 * q + 4, :].bitcast(I32), in_=w1_scales[0, 4 * q : 4 * q + 4, :].bitcast(I32))
+        for order, (j, on_vector, chunks) in enumerate(PLANES):
             for start, width, on_scalar in spans(chunks):
                 nc.sync.dma_start(out=planes[j][:, start : start + width], in_=rows[:, j, start : start + width])
-
-        load_plane(2, PLANE2_LOADS)
-        nc.sync.dma_start(picks[:], offs)
-        raws = []
-        for start, width, on_scalar in spans(PAIR_LOADS):
-            raw = keep.tile([P, 2, width], F32, name=f"raw{start}")
-            nc.sync.dma_start(out=raw[:], in_=rows[:, 0:2, start : start + width])
-            raws.append(raw)
-        load_plane(3, PLANE3_LOADS)
+            if order == 0:
+                nc.sync.dma_start(picks[:], offs)
         nc.sync.dma_start(out=w_words[:].bitcast(I32), in_=w1_words[0].rearrange("p n t -> p (n t)").bitcast(I32))
-        for q in range(4):
-            nc.sync.dma_start(out=w_scales[32 * q : 32 * q + 4, :].bitcast(I32), in_=w1_scales[0, 4 * q : 4 * q + 4, :].bitcast(I32))
         nc.sync.dma_start(owners[:], own)
         nc.sync.dma_start(out=res_sb[:], in_=res)
 
-        pairs = keep.tile([P, 2 * T], BF16, name="pairs", align_bytes=64)
-        n_picks = S // PICK
-        last = n_picks - 1
-        woven = [keep.tile([P, 4 * PICK], BF16, name=f"woven{c}", align_bytes=64) for c in range(n_picks)]
-        blocks = [(c, 0, PICK) for c in range(last)] + [(last, 0, PICK // 2), (last, PICK // 2, PICK // 2)]
-
-        def shared_round(dst, src, width, on_scalar):
-            if on_scalar > 0:
-                nc.scalar.activation(out=dst[:, :on_scalar], in_=src[:, :on_scalar], func=COPY)
-            if on_scalar < width:
-                nc.vector.tensor_copy(out=dst[:, on_scalar:], in_=src[:, on_scalar:])
-
         def round_plane(j, chunks):
             for start, width, on_scalar in spans(chunks):
-                shared_round(rounded[j][:, start : start + width], planes[j][:, start : start + width], width, on_scalar)
+                cut = start + on_scalar
+                if on_scalar > 0:
+                    nc.scalar.activation(out=rounded[j][:, start:cut], in_=planes[j][:, start:cut], func=COPY)
+                nc.vector.tensor_copy(out=rounded[j][:, cut : start + width], in_=planes[j][:, cut : start + width])
 
-        def round_pairs():
-            for (start, width, on_scalar), raw in zip(spans(PAIR_LOADS), raws):
-                dst = pairs[:, 2 * start : 2 * (start + width)].rearrange("p (c e) -> p c e", e=2)
-                shared_round(dst, raw[:].rearrange("p e c -> p c e"), width, on_scalar)
+        def slot(j, first, end):
+            return woven[:, 4 * first : 4 * end].rearrange("p (n t) -> p n t", t=4)[:, :, j]
 
-        def entries(c):
-            cols = PICK // LIST_ROWS
-            return picks[:, c * cols : (c + 1) * cols]
+        def entries(first, end):
+            return picks[:, first // LIST_ROWS : end // LIST_ROWS]
 
-        def gather_plane(j, c):
-            dst = woven[c][:].rearrange("p (n t) -> p n t", t=4)[:, :, j]
-            if c == 0:
-                nc.vector.tensor_copy(out=dst, in_=planes[j][:].indirect(entries(c)))
+        for order, (j, on_vector, chunks) in enumerate(PLANES):
+            round_plane(j, chunks)
+            nc.vector.tensor_copy(out=slot(j, 0, on_vector), in_=planes[j][:].indirect(entries(0, on_vector)))
+            cuts = (on_vector, LAST_CUT, S) if order == len(PLANES) - 1 else (on_vector, S)
+            for first, end in zip(cuts, cuts[1:]):
+                nc.scalar.activation(out=slot(j, first, end), in_=rounded[j][:].indirect(entries(first, end)), func=COPY)
+
+        for b, groups in enumerate(BANKS):
+            first = groups[0][0]
+            end = groups[-1][0] + groups[-1][1]
+            bank = psum.tile([P, end - first], F32, name=f"bank{b}")
+            for start, width in groups:
+                codes = keep.tile([P, width], U32, name=f"codes{start}", align_bytes=64)
+                scales = keep.tile([P, width], U8, name=f"scales{start}", align_bytes=64)
+                nc.vector.quantize_mx(out=codes[:].bitcast(FP8X4), scales=scales[:], in_=woven[:, 4 * start : 4 * (start + width)])
+                nc.tensor.matmul_mx(
+                    out=bank[:, start - first : start - first + width],
+                    lhsT=w_words[:].bitcast(FP8X4),
+                    lhsT_scale=w_scales[:],
+                    rhs=codes[:].bitcast(FP8X4),
+                    rhs_scale=scales[:],
+                    start=True,
+                    stop=True,
+                )
+            if b >= 2:
+                nc.vector.tensor_scalar_max(out=y[:, first:end], in0=bank[:], scalar1=0.0)
             else:
-                nc.scalar.activation(out=dst, in_=rounded[j][:].indirect(entries(c)), func=COPY)
-
-        def gather_pairs(c):
-            dst = woven[c][:].bitcast(U32).rearrange("p (n u) -> p n u", u=2)[:, :, 0]
-            nc.vector.tensor_copy(out=dst, in_=pairs[:].bitcast(U32).indirect(entries(c)))
-
-        def multiply(b):
-            c, start, width = blocks[b]
-            codes = keep.tile([P, width], U32, name=f"codes{b}", align_bytes=64)
-            scales = keep.tile([P, width], U8, name=f"scales{b}", align_bytes=64)
-            bank = psum.tile([P, width], F32, name=f"bank{b}")
-            nc.vector.quantize_mx(out=codes[:].bitcast(FP8X4), scales=scales[:], in_=woven[c][:, 4 * start : 4 * (start + width)])
-            nc.tensor.matmul_mx(
-                out=bank[:],
-                lhsT=w_words[:].bitcast(FP8X4),
-                lhsT_scale=w_scales[:],
-                rhs=codes[:].bitcast(FP8X4),
-                rhs_scale=scales[:],
-                start=True,
-                stop=True,
-            )
-            dst = y[:, c * PICK + start : c * PICK + start + width]
-            if b == len(blocks) - 1:
-                nc.vector.tensor_scalar_max(out=dst, in0=bank[:], scalar1=0.0)
-            else:
-                nc.scalar.activation(out=dst, in_=bank[:], func=RELU)
-
-        round_plane(2, PLANE2_LOADS)
-        for c in range(n_picks):
-            gather_plane(2, c)
-        round_pairs()
-        for c in list(range(1, n_picks)) + [0]:
-            gather_pairs(c)
-        round_plane(3, PLANE3_LOADS)
-        for c in range(n_picks):
-            gather_plane(3, c)
-        for b in range(len(blocks)):
-            multiply(b)
+                nc.scalar.activation(out=y[:, first:end], in_=bank[:], func=RELU)
 
         start = 0
         for width in OUT_WIDTHS:

@@ -25,7 +25,13 @@ PLANES = (
     (3, 384, ((1024, 0), (768, 0), (256, 0))),
 )
 LAST_CUT = 768
-BANKS = (((0, 256), (256, 128)), ((384, 256), (640, 128)), ((768, 128),), ((896, 128),))
+BANKS = (
+    ("scalar", ((0, 256), (256, 128))),
+    ("scalar", ((384, 256),)),
+    ("vector", ((640, 128),)),
+    ("vector", ((768, 128),)),
+    ("scalar", ((896, 128),)),
+)
 OUT_WIDTHS = (864, 576, 320, 192, 96)
 
 
@@ -87,7 +93,8 @@ def tile_picked_unmerge_relu_e_kernel(tc, xT, w1_words, w1_scales, res, offs, ow
             for first, end in zip(cuts, cuts[1:]):
                 nc.scalar.activation(out=slot(j, first, end), in_=rounded[j][:].indirect(entries(first, end)), func=COPY)
 
-        for b, groups in enumerate(BANKS):
+        filled = []
+        for b, (engine, groups) in enumerate(BANKS):
             first = groups[0][0]
             end = groups[-1][0] + groups[-1][1]
             bank = psum.tile([P, end - first], F32, name=f"bank{b}")
@@ -104,7 +111,9 @@ def tile_picked_unmerge_relu_e_kernel(tc, xT, w1_words, w1_scales, res, offs, ow
                     start=True,
                     stop=True,
                 )
-            if b >= 2:
+            filled.append((engine, first, end, bank))
+        for engine, first, end, bank in filled:
+            if engine == "vector":
                 nc.vector.tensor_scalar_max(out=y[:, first:end], in0=bank[:], scalar1=0.0)
             else:
                 nc.scalar.activation(out=y[:, first:end], in_=bank[:], func=RELU)

@@ -19,9 +19,9 @@ ADD = mybir.AluOpType.add
 P = 128
 LIST_ROWS = 16
 PLANES = (
-    (2, 384, ((1024, 384), (1024, 384))),
-    (0, 352, ((1024, 0), (1024, 0))),
-    (1, 352, ((1024, 0), (512, 0), (512, 0))),
+    (2, 384, ((1536, 512), (512, 160))),
+    (0, 352, ((1408, 0), (640, 192))),
+    (1, 352, ((1408, 0), (640, 0))),
     (3, 384, ((1024, 0), (768, 0), (256, 0))),
 )
 LAST_CUT = 768

@@ -19,20 +19,19 @@ ADD = mybir.AluOpType.add
 P = 128
 LIST_ROWS = 16
 PLANES = (
-    (2, 384, ((1536, 512), (512, 160))),
-    (0, 352, ((1408, 0), (640, 192))),
-    (1, 352, ((1408, 0), (640, 0))),
-    (3, 384, ((1024, 0), (768, 0), (256, 0))),
+    (2, (0, 384), ((384, 1024),), ((1536, 512), (512, 160))),
+    (0, (0, 320), ((320, 1024),), ((1408, 0), (640, 0))),
+    (1, (0, 320), ((320, 1024),), ((1408, 0), (640, 0))),
+    (3, (0, 384), ((384, 768), (768, 1024)), ((1152, 0), (640, 0), (256, 0))),
 )
-LAST_CUT = 768
-BANKS = (
-    ("scalar", ((0, 256), (256, 128))),
-    ("scalar", ((384, 256),)),
-    ("vector", ((640, 128),)),
-    ("vector", ((768, 128),)),
-    ("scalar", ((896, 128),)),
+BLOCKS = (
+    (0, 256, "scalar"),
+    (256, 256, "scalar"),
+    (512, 256, "vector"),
+    (768, 128, "scalar"),
+    (896, 128, "scalar"),
 )
-OUT_WIDTHS = (864, 576, 320, 192, 96)
+OUT_WIDTHS = (832, 576, 320, 192, 128)
 
 
 def tile_picked_unmerge_relu_e_kernel(tc, xT, w1_words, w1_scales, res, offs, own, out):
@@ -64,8 +63,8 @@ def tile_picked_unmerge_relu_e_kernel(tc, xT, w1_words, w1_scales, res, offs, ow
         nc.vector.memset(w_scales[:].bitcast(I32), 0)
         for q in range(4):
             nc.scalar.dma_start(out=w_scales[32 * q : 32 * q + 4, :].bitcast(I32), in_=w1_scales[0, 4 * q : 4 * q + 4, :].bitcast(I32))
-        for order, (j, on_vector, chunks) in enumerate(PLANES):
-            for start, width, on_scalar in spans(chunks):
+        for order, (j, on_vector, on_scalar, chunks) in enumerate(PLANES):
+            for start, width, helped in spans(chunks):
                 nc.sync.dma_start(out=planes[j][:, start : start + width], in_=rows[:, j, start : start + width])
             if order == 0:
                 nc.sync.dma_start(picks[:], offs)
@@ -74,11 +73,12 @@ def tile_picked_unmerge_relu_e_kernel(tc, xT, w1_words, w1_scales, res, offs, ow
         nc.sync.dma_start(out=res_sb[:], in_=res)
 
         def round_plane(j, chunks):
-            for start, width, on_scalar in spans(chunks):
-                cut = start + on_scalar
-                if on_scalar > 0:
+            for start, width, helped in spans(chunks):
+                cut = start + helped
+                if helped > 0:
                     nc.scalar.activation(out=rounded[j][:, start:cut], in_=planes[j][:, start:cut], func=COPY)
-                nc.vector.tensor_copy(out=rounded[j][:, cut : start + width], in_=planes[j][:, cut : start + width])
+                if helped < width:
+                    nc.vector.tensor_copy(out=rounded[j][:, cut : start + width], in_=planes[j][:, cut : start + width])
 
         def slot(j, first, end):
             return woven[:, 4 * first : 4 * end].rearrange("p (n t) -> p n t", t=4)[:, :, j]
@@ -86,32 +86,28 @@ def tile_picked_unmerge_relu_e_kernel(tc, xT, w1_words, w1_scales, res, offs, ow
         def entries(first, end):
             return picks[:, first // LIST_ROWS : end // LIST_ROWS]
 
-        for order, (j, on_vector, chunks) in enumerate(PLANES):
+        for j, on_vector, on_scalar, chunks in PLANES:
             round_plane(j, chunks)
-            nc.vector.tensor_copy(out=slot(j, 0, on_vector), in_=planes[j][:].indirect(entries(0, on_vector)))
-            cuts = (on_vector, LAST_CUT, S) if order == len(PLANES) - 1 else (on_vector, S)
-            for first, end in zip(cuts, cuts[1:]):
+            nc.vector.tensor_copy(out=slot(j, *on_vector), in_=planes[j][:].indirect(entries(*on_vector)))
+            for first, end in on_scalar:
                 nc.scalar.activation(out=slot(j, first, end), in_=rounded[j][:].indirect(entries(first, end)), func=COPY)
 
         filled = []
-        for b, (engine, groups) in enumerate(BANKS):
-            first = groups[0][0]
-            end = groups[-1][0] + groups[-1][1]
-            bank = psum.tile([P, end - first], F32, name=f"bank{b}")
-            for start, width in groups:
-                codes = keep.tile([P, width], U32, name=f"codes{start}", align_bytes=64)
-                scales = keep.tile([P, width], U8, name=f"scales{start}", align_bytes=64)
-                nc.vector.quantize_mx(out=codes[:].bitcast(FP8X4), scales=scales[:], in_=woven[:, 4 * start : 4 * (start + width)])
-                nc.tensor.matmul_mx(
-                    out=bank[:, start - first : start - first + width],
-                    lhsT=w_words[:].bitcast(FP8X4),
-                    lhsT_scale=w_scales[:],
-                    rhs=codes[:].bitcast(FP8X4),
-                    rhs_scale=scales[:],
-                    start=True,
-                    stop=True,
-                )
-            filled.append((engine, first, end, bank))
+        for start, width, engine in BLOCKS:
+            bank = psum.tile([P, width], F32, name=f"bank{start}")
+            codes = keep.tile([P, width], U32, name=f"codes{start}", align_bytes=64)
+            scales = keep.tile([P, width], U8, name=f"scales{start}", align_bytes=64)
+            nc.vector.quantize_mx(out=codes[:].bitcast(FP8X4), scales=scales[:], in_=woven[:, 4 * start : 4 * (start + width)])
+            nc.tensor.matmul_mx(
+                out=bank[:],
+                lhsT=w_words[:].bitcast(FP8X4),
+                lhsT_scale=w_scales[:],
+                rhs=codes[:].bitcast(FP8X4),
+                rhs_scale=scales[:],
+                start=True,
+                stop=True,
+            )
+            filled.append((engine, start, start + width, bank))
         for engine, first, end, bank in filled:
             if engine == "vector":
                 nc.vector.tensor_scalar_max(out=y[:, first:end], in0=bank[:], scalar1=0.0)

@@ -19,10 +19,10 @@ ADD = mybir.AluOpType.add
 P = 128
 LIST_ROWS = 16
 PLANES = (
-    (2, (0, 384), ((384, 1024),), ((1536, 512), (512, 160))),
+    (2, (0, 416), ((416, 1024),), ((1536, 512), (512, 160))),
     (0, (0, 320), ((320, 1024),), ((1408, 0), (640, 0))),
     (1, (0, 320), ((320, 1024),), ((1408, 0), (640, 0))),
-    (3, (0, 384), ((384, 768), (768, 1024)), ((1152, 0), (640, 0), (256, 0))),
+    (3, (0, 416), ((416, 768), (768, 1024)), ((1152, 0), (640, 0), (256, 0))),
 )
 BLOCKS = (
     (0, 256, "scalar"),

@@ -19,10 +19,10 @@ ADD = mybir.AluOpType.add
 P = 128
 LIST_ROWS = 16
 PLANES = (
-    (2, (0, 416), ((416, 1024),), ((1536, 512), (512, 160))),
+    (2, (0, 448), ((448, 1024),), ((1536, 512), (512, 160))),
     (0, (0, 320), ((320, 1024),), ((1408, 0), (640, 0))),
     (1, (0, 320), ((320, 1024),), ((1408, 0), (640, 0))),
-    (3, (0, 416), ((416, 768), (768, 1024)), ((1152, 0), (640, 0), (256, 0))),
+    (3, (0, 448), ((448, 768), (768, 1024)), ((1152, 0), (640, 0), (256, 0))),
 )
 BLOCKS = (
     (0, 256, "scalar"),

@@ -31,7 +31,8 @@ BLOCKS = (
     (768, 128, "scalar"),
     (896, 128, "scalar"),
 )
-OUT_WIDTHS = (832, 576, 320, 192, 128)
+FUSED_WIDTHS = (384, 384)
+FETCHED_WIDTHS = (448, 352, 256, 128, 96)
 
 
 def tile_picked_unmerge_relu_e_kernel(tc, xT, w1_words, w1_scales, res, offs, own, out):
@@ -114,10 +115,19 @@ def tile_picked_unmerge_relu_e_kernel(tc, xT, w1_words, w1_scales, res, offs, ow
             else:
                 nc.scalar.activation(out=y[:, first:end], in_=bank[:], func=RELU)
 
+        def owned(start, width):
+            return y[:].indirect(owners[:, start // LIST_ROWS : (start + width) // LIST_ROWS])
+
         start = 0
-        for width in OUT_WIDTHS:
+        for width in FUSED_WIDTHS:
             summed = keep.tile([P, width], F32, name=f"summed{start}")
-            window = y[:].indirect(owners[:, start // LIST_ROWS : (start + width) // LIST_ROWS])
-            nc.vector.tensor_tensor(out=summed[:], in0=window, in1=res_sb[:, start : start + width], op=ADD)
+            nc.vector.tensor_tensor(out=summed[:], in0=owned(start, width), in1=res_sb[:, start : start + width], op=ADD)
+            nc.sync.dma_start(out=out[:, start : start + width], in_=summed[:])
+            start += width
+        for width in FETCHED_WIDTHS:
+            fetched = keep.tile([P, width], F32, name=f"fetched{start}")
+            summed = keep.tile([P, width], F32, name=f"summed{start}")
+            nc.scalar.activation(out=fetched[:], in_=owned(start, width), func=COPY)
+            nc.vector.tensor_tensor(out=summed[:], in0=fetched[:], in1=res_sb[:, start : start + width], op=ADD)
             nc.sync.dma_start(out=out[:, start : start + width], in_=summed[:])
             start += width

@@ -19,20 +19,22 @@ ADD = mybir.AluOpType.add
 P = 128
 LIST_ROWS = 16
 PLANES = (
-    (2, (0, 448), ((448, 1024),), ((1536, 512), (512, 160))),
-    (0, (0, 320), ((320, 1024),), ((1408, 0), (640, 0))),
-    (1, (0, 320), ((320, 1024),), ((1408, 0), (640, 0))),
-    (3, (0, 448), ((448, 768), (768, 1024)), ((1152, 0), (640, 0), (256, 0))),
+    (2, 512, ((832, 960), (960, 1024),), ((512, 640), (640, 832),)),
+    (0, 640, ((640, 768), (768, 1024),), ()),
+    (1, 640, ((640, 768), (768, 1024),), ()),
+    (3, 512, ((832, 960), (960, 1024),), ((512, 640), (640, 832),)),
 )
 BLOCKS = (
+    (832, 128, "scalar"),
+    (960, 64, "scalar"),
     (0, 256, "scalar"),
-    (256, 256, "scalar"),
-    (512, 256, "vector"),
-    (768, 128, "scalar"),
-    (896, 128, "scalar"),
+    (256, 256, "vector"),
+    (512, 128, "scalar"),
+    (640, 128, "scalar"),
+    (768, 64, "vector"),
 )
-FUSED_WIDTHS = (384, 384)
-FETCHED_WIDTHS = (448, 352, 256, 128, 96)
+FUSED_WIDTHS = (384, 384,)
+FETCHED_WIDTHS = (448, 352, 256, 128, 96,)
 
 
 def tile_picked_unmerge_relu_e_kernel(tc, xT, w1_words, w1_scales, res, offs, own, out):
@@ -50,36 +52,21 @@ def tile_picked_unmerge_relu_e_kernel(tc, xT, w1_words, w1_scales, res, offs, ow
         y = keep.tile([P, S], F32, name="y")
 
         planes = [keep.tile([P, T], F32, name=f"plane{j}") for j in range(4)]
-        rounded = [keep.tile([P, T], BF16, name=f"rounded{j}") for j in range(4)]
         woven = keep.tile([P, 4 * S], BF16, name="woven", align_bytes=64)
 
-        def spans(chunks):
-            start = 0
-            found = []
-            for width, on_scalar in chunks:
-                found.append((start, width, on_scalar))
-                start += width
-            return found
-
         nc.vector.memset(w_scales[:].bitcast(I32), 0)
+        idle = keep.tile([P, 2], F32, name="idle")
+        nc.vector.memset(idle[:, 0:1], 0.0)
+        nc.scalar.activation(out=idle[:, 1:2], in_=idle[:, 0:1], func=COPY)
         for q in range(4):
             nc.scalar.dma_start(out=w_scales[32 * q : 32 * q + 4, :].bitcast(I32), in_=w1_scales[0, 4 * q : 4 * q + 4, :].bitcast(I32))
-        for order, (j, on_vector, on_scalar, chunks) in enumerate(PLANES):
-            for start, width, helped in spans(chunks):
-                nc.sync.dma_start(out=planes[j][:, start : start + width], in_=rows[:, j, start : start + width])
+        for order, (j, on_vector, by_gpsimd, by_scalar) in enumerate(PLANES):
+            nc.sync.dma_start(out=planes[j][:], in_=rows[:, j, :])
             if order == 0:
                 nc.sync.dma_start(picks[:], offs)
         nc.sync.dma_start(out=w_words[:].bitcast(I32), in_=w1_words[0].rearrange("p n t -> p (n t)").bitcast(I32))
         nc.sync.dma_start(owners[:], own)
         nc.sync.dma_start(out=res_sb[:], in_=res)
-
-        def round_plane(j, chunks):
-            for start, width, helped in spans(chunks):
-                cut = start + helped
-                if helped > 0:
-                    nc.scalar.activation(out=rounded[j][:, start:cut], in_=planes[j][:, start:cut], func=COPY)
-                if helped < width:
-                    nc.vector.tensor_copy(out=rounded[j][:, cut : start + width], in_=planes[j][:, cut : start + width])
 
         def slot(j, first, end):
             return woven[:, 4 * first : 4 * end].rearrange("p (n t) -> p n t", t=4)[:, :, j]
@@ -87,23 +74,35 @@ def tile_picked_unmerge_relu_e_kernel(tc, xT, w1_words, w1_scales, res, offs, ow
         def entries(first, end):
             return picks[:, first // LIST_ROWS : end // LIST_ROWS]
 
-        for j, on_vector, on_scalar, chunks in PLANES:
-            round_plane(j, chunks)
-            nc.vector.tensor_copy(out=slot(j, *on_vector), in_=planes[j][:].indirect(entries(*on_vector)))
-            for first, end in on_scalar:
-                nc.scalar.activation(out=slot(j, first, end), in_=rounded[j][:].indirect(entries(first, end)), func=COPY)
+        for j, on_vector, by_gpsimd, by_scalar in PLANES:
+            nc.vector.tensor_copy(out=slot(j, 0, on_vector), in_=planes[j][:].indirect(entries(0, on_vector)))
+            staged = []
+            for first, end in by_gpsimd + by_scalar:
+                tag = "reused" if (j, end) == (PLANES[-1][0], S) else f"piece{j}_{first}"
+                piece = keep.tile([P, end - first], BF16, name=f"piece{j}_{first}", tag=tag, align_bytes=64)
+                nc.scalar.activation(out=piece[:], in_=planes[j][:].indirect(entries(first, end)), func=COPY)
+                staged.append(piece)
+            for (first, end), piece in zip(by_gpsimd, staged):
+                nc.gpsimd.tensor_copy(out=slot(j, first, end), in_=piece[:])
+            for (first, end), piece in zip(by_scalar, staged[len(by_gpsimd) :]):
+                nc.scalar.copy(out=slot(j, first, end), in_=piece[:])
 
+        head = PLANES[-1][1]
+        head_codes = keep.tile([P, head], U32, name="head_codes", tag="reused", align_bytes=64)
         filled = []
         for start, width, engine in BLOCKS:
             bank = psum.tile([P, width], F32, name=f"bank{start}")
-            codes = keep.tile([P, width], U32, name=f"codes{start}", align_bytes=64)
+            if start < head:
+                codes = head_codes[:, start : start + width]
+            else:
+                codes = keep.tile([P, width], U32, name=f"codes{start}", align_bytes=64)[:]
             scales = keep.tile([P, width], U8, name=f"scales{start}", align_bytes=64)
-            nc.vector.quantize_mx(out=codes[:].bitcast(FP8X4), scales=scales[:], in_=woven[:, 4 * start : 4 * (start + width)])
+            nc.vector.quantize_mx(out=codes.bitcast(FP8X4), scales=scales[:], in_=woven[:, 4 * start : 4 * (start + width)])
             nc.tensor.matmul_mx(
                 out=bank[:],
                 lhsT=w_words[:].bitcast(FP8X4),
                 lhsT_scale=w_scales[:],
-                rhs=codes[:].bitcast(FP8X4),
+                rhs=codes.bitcast(FP8X4),
                 rhs_scale=scales[:],
                 start=True,
                 stop=True,

@@ -19,19 +19,18 @@ ADD = mybir.AluOpType.add
 P = 128
 LIST_ROWS = 16
 PLANES = (
-    (2, 512, ((832, 960), (960, 1024),), ((512, 640), (640, 832),)),
+    (2, 512, ((864, 1024),), ((512, 768), (768, 864),)),
     (0, 640, ((640, 768), (768, 1024),), ()),
     (1, 640, ((640, 768), (768, 1024),), ()),
-    (3, 512, ((832, 960), (960, 1024),), ((512, 640), (640, 832),)),
+    (3, 512, ((864, 1024),), ((512, 768), (768, 864),)),
 )
 BLOCKS = (
-    (832, 128, "scalar"),
-    (960, 64, "scalar"),
     (0, 256, "scalar"),
-    (256, 256, "vector"),
-    (512, 128, "scalar"),
+    (256, 256, "scalar"),
+    (896, 128, "vector"),
+    (512, 128, "vector"),
     (640, 128, "scalar"),
-    (768, 64, "vector"),
+    (768, 128, "vector"),
 )
 FUSED_WIDTHS = (384, 384,)
 FETCHED_WIDTHS = (448, 352, 256, 128, 96,)
@@ -75,11 +74,12 @@ def tile_picked_unmerge_relu_e_kernel(tc, xT, w1_words, w1_scales, res, offs, ow
             return picks[:, first // LIST_ROWS : end // LIST_ROWS]
 
         for j, on_vector, by_gpsimd, by_scalar in PLANES:
-            nc.vector.tensor_copy(out=slot(j, 0, on_vector), in_=planes[j][:].indirect(entries(0, on_vector)))
+            cuts = (0, on_vector // 2, on_vector) if j == PLANES[-1][0] else (0, on_vector)
+            for first, end in zip(cuts, cuts[1:]):
+                nc.vector.tensor_copy(out=slot(j, first, end), in_=planes[j][:].indirect(entries(first, end)))
             staged = []
             for first, end in by_gpsimd + by_scalar:
-                tag = "reused" if (j, end) == (PLANES[-1][0], S) else f"piece{j}_{first}"
-                piece = keep.tile([P, end - first], BF16, name=f"piece{j}_{first}", tag=tag, align_bytes=64)
+                piece = keep.tile([P, end - first], BF16, name=f"piece{j}_{first}")
                 nc.scalar.activation(out=piece[:], in_=planes[j][:].indirect(entries(first, end)), func=COPY)
                 staged.append(piece)
             for (first, end), piece in zip(by_gpsimd, staged):
@@ -87,22 +87,17 @@ def tile_picked_unmerge_relu_e_kernel(tc, xT, w1_words, w1_scales, res, offs, ow
             for (first, end), piece in zip(by_scalar, staged[len(by_gpsimd) :]):
                 nc.scalar.copy(out=slot(j, first, end), in_=piece[:])
 
-        head = PLANES[-1][1]
-        head_codes = keep.tile([P, head], U32, name="head_codes", tag="reused", align_bytes=64)
         filled = []
         for start, width, engine in BLOCKS:
             bank = psum.tile([P, width], F32, name=f"bank{start}")
-            if start < head:
-                codes = head_codes[:, start : start + width]
-            else:
-                codes = keep.tile([P, width], U32, name=f"codes{start}", align_bytes=64)[:]
+            codes = keep.tile([P, width], U32, name=f"codes{start}", align_bytes=64)
             scales = keep.tile([P, width], U8, name=f"scales{start}", align_bytes=64)
-            nc.vector.quantize_mx(out=codes.bitcast(FP8X4), scales=scales[:], in_=woven[:, 4 * start : 4 * (start + width)])
+            nc.vector.quantize_mx(out=codes[:].bitcast(FP8X4), scales=scales[:], in_=woven[:, 4 * start : 4 * (start + width)])
             nc.tensor.matmul_mx(
                 out=bank[:],
                 lhsT=w_words[:].bitcast(FP8X4),
                 lhsT_scale=w_scales[:],
-                rhs=codes.bitcast(FP8X4),
+                rhs=codes[:].bitcast(FP8X4),
                 rhs_scale=scales[:],
                 start=True,
                 stop=True,

@@ -19,7 +19,7 @@ ADD = mybir.AluOpType.add
 P = 128
 LIST_ROWS = 16
 PLANES = (
-    (2, 512, ((864, 1024),), ((512, 768), (768, 864),)),
+    (2, 512, ((864, 1024), (640, 864),), ((512, 640),)),
     (0, 640, ((640, 768), (768, 1024),), ()),
     (1, 640, ((640, 768), (768, 1024),), ()),
     (3, 512, ((864, 1024),), ((512, 768), (768, 864),)),
@@ -32,8 +32,7 @@ BLOCKS = (
     (640, 128, "scalar"),
     (768, 128, "vector"),
 )
-FUSED_WIDTHS = (384, 384,)
-FETCHED_WIDTHS = (448, 352, 256, 128, 96,)
+OUT_PIECES = (("vector", 384), ("scalar", 224), ("vector", 192), ("scalar", 320), ("vector", 192), ("scalar", 352), ("vector", 128), ("scalar", 256))
 
 
 def tile_picked_unmerge_relu_e_kernel(tc, xT, w1_words, w1_scales, res, offs, own, out):
@@ -54,16 +53,13 @@ def tile_picked_unmerge_relu_e_kernel(tc, xT, w1_words, w1_scales, res, offs, ow
         woven = keep.tile([P, 4 * S], BF16, name="woven", align_bytes=64)
 
         nc.vector.memset(w_scales[:].bitcast(I32), 0)
-        idle = keep.tile([P, 2], F32, name="idle")
-        nc.vector.memset(idle[:, 0:1], 0.0)
-        nc.scalar.activation(out=idle[:, 1:2], in_=idle[:, 0:1], func=COPY)
-        for q in range(4):
-            nc.scalar.dma_start(out=w_scales[32 * q : 32 * q + 4, :].bitcast(I32), in_=w1_scales[0, 4 * q : 4 * q + 4, :].bitcast(I32))
         for order, (j, on_vector, by_gpsimd, by_scalar) in enumerate(PLANES):
             nc.sync.dma_start(out=planes[j][:], in_=rows[:, j, :])
             if order == 0:
                 nc.sync.dma_start(picks[:], offs)
         nc.sync.dma_start(out=w_words[:].bitcast(I32), in_=w1_words[0].rearrange("p n t -> p (n t)").bitcast(I32))
+        for q in range(4):
+            nc.sync.dma_start(out=w_scales[32 * q : 32 * q + 4, :].bitcast(I32), in_=w1_scales[0, 4 * q : 4 * q + 4, :].bitcast(I32))
         nc.sync.dma_start(owners[:], own)
         nc.sync.dma_start(out=res_sb[:], in_=res)
 
@@ -78,8 +74,9 @@ def tile_picked_unmerge_relu_e_kernel(tc, xT, w1_words, w1_scales, res, offs, ow
             for first, end in zip(cuts, cuts[1:]):
                 nc.vector.tensor_copy(out=slot(j, first, end), in_=planes[j][:].indirect(entries(first, end)))
             staged = []
-            for first, end in by_gpsimd + by_scalar:
-                piece = keep.tile([P, end - first], BF16, name=f"piece{j}_{first}")
+            for place, (first, end) in enumerate(by_gpsimd + by_scalar):
+                tag = "shared" if j >= 2 and place == 1 else f"piece{j}_{first}"
+                piece = keep.tile([P, end - first], BF16, name=f"piece{j}_{first}", tag=tag)
                 nc.scalar.activation(out=piece[:], in_=planes[j][:].indirect(entries(first, end)), func=COPY)
                 staged.append(piece)
             for (first, end), piece in zip(by_gpsimd, staged):
@@ -113,15 +110,13 @@ def tile_picked_unmerge_relu_e_kernel(tc, xT, w1_words, w1_scales, res, offs, ow
             return y[:].indirect(owners[:, start // LIST_ROWS : (start + width) // LIST_ROWS])
 
         start = 0
-        for width in FUSED_WIDTHS:
+        for fetcher, width in OUT_PIECES:
             summed = keep.tile([P, width], F32, name=f"summed{start}")
-            nc.vector.tensor_tensor(out=summed[:], in0=owned(start, width), in1=res_sb[:, start : start + width], op=ADD)
-            nc.sync.dma_start(out=out[:, start : start + width], in_=summed[:])
-            start += width
-        for width in FETCHED_WIDTHS:
-            fetched = keep.tile([P, width], F32, name=f"fetched{start}")
-            summed = keep.tile([P, width], F32, name=f"summed{start}")
-            nc.scalar.activation(out=fetched[:], in_=owned(start, width), func=COPY)
-            nc.vector.tensor_tensor(out=summed[:], in0=fetched[:], in1=res_sb[:, start : start + width], op=ADD)
+            addend = owned(start, width)
+            if fetcher == "scalar":
+                fetched = keep.tile([P, width], F32, name=f"fetched{start}")
+                nc.scalar.activation(out=fetched[:], in_=addend, func=COPY)
+                addend = fetched[:]
+            nc.vector.tensor_tensor(out=summed[:], in0=addend, in1=res_sb[:, start : start + width], op=ADD)
             nc.sync.dma_start(out=out[:, start : start + width], in_=summed[:])
             start += width

@@ -19,18 +19,18 @@ ADD = mybir.AluOpType.add
 P = 128
 LIST_ROWS = 16
 PLANES = (
-    (2, 512, ((864, 1024), (640, 864),), ((512, 640),)),
-    (0, 640, ((640, 768), (768, 1024),), ()),
-    (1, 640, ((640, 768), (768, 1024),), ()),
-    (3, 512, ((864, 1024),), ((512, 768), (768, 864),)),
+    (0, 640, ((640, 768), (768, 1024),), ((640, 768), (768, 1024),), ()),
+    (1, 640, ((640, 768), (768, 1024),), ((640, 768), (768, 1024),), ()),
+    (2, 512, ((832, 1024), (640, 832), (512, 640),), ((832, 1024), (640, 832),), ((512, 640),)),
+    (3, 512, ((832, 1024), (512, 672), (672, 832),), ((832, 1024),), ((512, 640), (640, 768), (768, 832),)),
 )
 BLOCKS = (
-    (0, 256, "scalar"),
-    (256, 256, "scalar"),
-    (896, 128, "vector"),
-    (512, 128, "vector"),
-    (640, 128, "scalar"),
-    (768, 128, "vector"),
+    (0, 256, ("scalar",)),
+    (256, 256, ("scalar",)),
+    (896, 128, ("vector",)),
+    (512, 128, ("vector",)),
+    (640, 128, ("scalar",)),
+    (768, 128, ("vector", "scalar",)),
 )
 OUT_PIECES = (("vector", 384), ("scalar", 224), ("vector", 192), ("scalar", 320), ("vector", 192), ("scalar", 352), ("vector", 128), ("scalar", 256))
 
@@ -53,7 +53,7 @@ def tile_picked_unmerge_relu_e_kernel(tc, xT, w1_words, w1_scales, res, offs, ow
         woven = keep.tile([P, 4 * S], BF16, name="woven", align_bytes=64)
 
         nc.vector.memset(w_scales[:].bitcast(I32), 0)
-        for order, (j, on_vector, by_gpsimd, by_scalar) in enumerate(PLANES):
+        for order, (j, *shares) in enumerate(PLANES):
             nc.sync.dma_start(out=planes[j][:], in_=rows[:, j, :])
             if order == 0:
                 nc.sync.dma_start(picks[:], offs)
@@ -69,37 +69,41 @@ def tile_picked_unmerge_relu_e_kernel(tc, xT, w1_words, w1_scales, res, offs, ow
         def entries(first, end):
             return picks[:, first // LIST_ROWS : end // LIST_ROWS]
 
-        for j, on_vector, by_gpsimd, by_scalar in PLANES:
+        for j, on_vector, gathered, by_gpsimd, by_scalar in PLANES:
             cuts = (0, on_vector // 2, on_vector) if j == PLANES[-1][0] else (0, on_vector)
             for first, end in zip(cuts, cuts[1:]):
                 nc.vector.tensor_copy(out=slot(j, first, end), in_=planes[j][:].indirect(entries(first, end)))
-            staged = []
-            for place, (first, end) in enumerate(by_gpsimd + by_scalar):
-                tag = "shared" if j >= 2 and place == 1 else f"piece{j}_{first}"
-                piece = keep.tile([P, end - first], BF16, name=f"piece{j}_{first}", tag=tag)
-                nc.scalar.activation(out=piece[:], in_=planes[j][:].indirect(entries(first, end)), func=COPY)
-                staged.append(piece)
-            for (first, end), piece in zip(by_gpsimd, staged):
-                nc.gpsimd.tensor_copy(out=slot(j, first, end), in_=piece[:])
-            for (first, end), piece in zip(by_scalar, staged[len(by_gpsimd) :]):
-                nc.scalar.copy(out=slot(j, first, end), in_=piece[:])
+            lead = keep.tile([P, S], BF16, name=f"lead{j}")
+            rest = keep.tile([P, S], BF16, name=f"rest{j}", tag=f"rest{min(j, 2)}")
+
+            def staged(first, end):
+                return (lead if first == gathered[0][0] else rest)[:, first:end]
+
+            for first, end in gathered:
+                nc.scalar.activation(out=staged(first, end), in_=planes[j][:].indirect(entries(first, end)), func=COPY)
+            for first, end in by_gpsimd:
+                nc.gpsimd.tensor_copy(out=slot(j, first, end), in_=staged(first, end))
+            for first, end in by_scalar:
+                nc.scalar.copy(out=slot(j, first, end), in_=staged(first, end))
 
         filled = []
-        for start, width, engine in BLOCKS:
-            bank = psum.tile([P, width], F32, name=f"bank{start}")
+        for start, width, engines in BLOCKS:
             codes = keep.tile([P, width], U32, name=f"codes{start}", align_bytes=64)
             scales = keep.tile([P, width], U8, name=f"scales{start}", align_bytes=64)
             nc.vector.quantize_mx(out=codes[:].bitcast(FP8X4), scales=scales[:], in_=woven[:, 4 * start : 4 * (start + width)])
-            nc.tensor.matmul_mx(
-                out=bank[:],
-                lhsT=w_words[:].bitcast(FP8X4),
-                lhsT_scale=w_scales[:],
-                rhs=codes[:].bitcast(FP8X4),
-                rhs_scale=scales[:],
-                start=True,
-                stop=True,
-            )
-            filled.append((engine, start, start + width, bank))
+            part = width // len(engines)
+            for first, engine in zip(range(0, width, part), engines):
+                bank = psum.tile([P, part], F32, name=f"bank{start + first}")
+                nc.tensor.matmul_mx(
+                    out=bank[:],
+                    lhsT=w_words[:].bitcast(FP8X4),
+                    lhsT_scale=w_scales[:],
+                    rhs=codes[:, first : first + part].bitcast(FP8X4),
+                    rhs_scale=scales[:, first : first + part],
+                    start=True,
+                    stop=True,
+                )
+                filled.append((engine, start + first, start + first + part, bank))
         for engine, first, end, bank in filled:
             if engine == "vector":
                 nc.vector.tensor_scalar_max(out=y[:, first:end], in0=bank[:], scalar1=0.0)

@@ -33,6 +33,7 @@ BLOCKS = (
     (768, 128, ("vector", "scalar",)),
 )
 OUT_PIECES = (("vector", 384), ("scalar", 224), ("vector", 192), ("scalar", 320), ("vector", 192), ("scalar", 352), ("vector", 128), ("scalar", 256))
+RES_CUTS = (0, 384, 608, 1120, 1664, 2048)
 
 
 def tile_picked_unmerge_relu_e_kernel(tc, xT, w1_words, w1_scales, res, offs, own, out):
@@ -61,7 +62,8 @@ def tile_picked_unmerge_relu_e_kernel(tc, xT, w1_words, w1_scales, res, offs, ow
         for q in range(4):
             nc.sync.dma_start(out=w_scales[32 * q : 32 * q + 4, :].bitcast(I32), in_=w1_scales[0, 4 * q : 4 * q + 4, :].bitcast(I32))
         nc.sync.dma_start(owners[:], own)
-        nc.sync.dma_start(out=res_sb[:], in_=res)
+        for first, end in zip(RES_CUTS, RES_CUTS[1:]):
+            nc.sync.dma_start(out=res_sb[:, first:end], in_=res[:, first:end])
 
         def slot(j, first, end):
             return woven[:, 4 * first : 4 * end].rearrange("p (n t) -> p n t", t=4)[:, :, j]

@@ -47,7 +47,6 @@ def tile_picked_unmerge_relu_e_kernel(tc, xT, w1_words, w1_scales, res, offs, ow
         owners = keep.tile([P, U // LIST_ROWS], U16, name="owners")
         w_words = keep.tile([P, M], U32, name="w_words", align_bytes=64)
         w_scales = keep.tile([P, M], U8, name="w_scales", align_bytes=64)
-        res_sb = keep.tile([P, U], F32, name="res_sb")
         y = keep.tile([P, S], F32, name="y")
 
         planes = [keep.tile([P, T], F32, name=f"plane{j}") for j in range(4)]
@@ -62,8 +61,6 @@ def tile_picked_unmerge_relu_e_kernel(tc, xT, w1_words, w1_scales, res, offs, ow
         for q in range(4):
             nc.sync.dma_start(out=w_scales[32 * q : 32 * q + 4, :].bitcast(I32), in_=w1_scales[0, 4 * q : 4 * q + 4, :].bitcast(I32))
         nc.sync.dma_start(owners[:], own)
-        for first, end in zip(RES_CUTS, RES_CUTS[1:]):
-            nc.sync.dma_start(out=res_sb[:, first:end], in_=res[:, first:end])
 
         def slot(j, first, end):
             return woven[:, 4 * first : 4 * end].rearrange("p (n t) -> p n t", t=4)[:, :, j]
@@ -87,6 +84,10 @@ def tile_picked_unmerge_relu_e_kernel(tc, xT, w1_words, w1_scales, res, offs, ow
                 nc.gpsimd.tensor_copy(out=slot(j, first, end), in_=staged(first, end))
             for first, end in by_scalar:
                 nc.scalar.copy(out=slot(j, first, end), in_=staged(first, end))
+
+        res_sb = keep.tile([P, U], F32, name="res_sb", tag=f"plane{PLANES[2][0]}")
+        for first, end in zip(RES_CUTS, RES_CUTS[1:]):
+            nc.sync.dma_start(out=res_sb[:, first:end], in_=res[:, first:end])
 
         filled = []
         for start, width, engines in BLOCKS:

@@ -19,19 +19,29 @@ ADD = mybir.AluOpType.add
 P = 128
 LIST_ROWS = 16
 PLANES = (
-    (0, 640, ((640, 768), (768, 1024),), ((640, 768), (768, 1024),), ()),
-    (1, 640, ((640, 768), (768, 1024),), ((640, 768), (768, 1024),), ()),
-    (2, 512, ((832, 1024), (640, 832), (512, 640),), ((832, 1024), (640, 832),), ((512, 640),)),
-    (3, 512, ((832, 1024), (512, 672), (672, 832),), ((832, 1024),), ((512, 640), (640, 768), (768, 832),)),
+    (640, (("a0", 640, 768, (("gpsimd", 640, 768),)), ("b0", 768, 1024, (("gpsimd", 768, 1024),)))),
+    (640, (("a1", 640, 768, (("gpsimd", 640, 768),)), ("b1", 768, 1024, (("gpsimd", 768, 1024),)))),
+    (512, (("a2", 832, 1024, (("gpsimd", 832, 1024),)), ("late", 640, 832, (("gpsimd", 640, 832),)), ("late", 512, 640, (("scalar", 512, 640),)))),
+    (
+        448,
+        (
+            ("a3", 832, 896, (("gpsimd", 832, 896),)),
+            ("b3", 896, 1024, (("gpsimd", 896, 1024),)),
+            ("late", 448, 640, (("vector", 448, 512), ("scalar", 512, 640))),
+            ("late", 640, 832, (("scalar", 640, 768), ("scalar", 768, 832))),
+        ),
+    ),
 )
-BLOCKS = (
-    (0, 256, ("scalar",)),
-    (256, 256, ("scalar",)),
-    (896, 128, ("vector",)),
-    (512, 128, ("vector",)),
-    (640, 128, ("scalar",)),
-    (768, 128, ("vector", "scalar",)),
+BANKS = (
+    (((832, 64),), "scalar"),
+    (((896, 128),), "scalar"),
+    (((0, 128), (128, 128)), "scalar"),
+    (((256, 128), (384, 128)), "vector"),
+    (((512, 128),), "scalar"),
+    (((640, 128),), "vector"),
+    (((768, 64),), "scalar"),
 )
+HEAD = 512
 OUT_PIECES = (("vector", 384), ("scalar", 224), ("vector", 192), ("scalar", 320), ("vector", 192), ("scalar", 352), ("vector", 128), ("scalar", 256))
 RES_CUTS = (0, 384, 608, 1120, 1664, 2048)
 
@@ -48,14 +58,13 @@ def tile_picked_unmerge_relu_e_kernel(tc, xT, w1_words, w1_scales, res, offs, ow
         w_words = keep.tile([P, M], U32, name="w_words", align_bytes=64)
         w_scales = keep.tile([P, M], U8, name="w_scales", align_bytes=64)
         y = keep.tile([P, S], F32, name="y")
-
         planes = [keep.tile([P, T], F32, name=f"plane{j}") for j in range(4)]
         woven = keep.tile([P, 4 * S], BF16, name="woven", align_bytes=64)
 
         nc.vector.memset(w_scales[:].bitcast(I32), 0)
-        for order, (j, *shares) in enumerate(PLANES):
+        for j in range(4):
             nc.sync.dma_start(out=planes[j][:], in_=rows[:, j, :])
-            if order == 0:
+            if j == 0:
                 nc.sync.dma_start(picks[:], offs)
         nc.sync.dma_start(out=w_words[:].bitcast(I32), in_=w1_words[0].rearrange("p n t -> p (n t)").bitcast(I32))
         for q in range(4):
@@ -65,61 +74,55 @@ def tile_picked_unmerge_relu_e_kernel(tc, xT, w1_words, w1_scales, res, offs, ow
         def slot(j, first, end):
             return woven[:, 4 * first : 4 * end].rearrange("p (n t) -> p n t", t=4)[:, :, j]
 
-        def entries(first, end):
-            return picks[:, first // LIST_ROWS : end // LIST_ROWS]
+        def picked(j, first, end):
+            return planes[j][:].indirect(picks[:, first // LIST_ROWS : end // LIST_ROWS])
 
-        for j, on_vector, gathered, by_gpsimd, by_scalar in PLANES:
-            cuts = (0, on_vector // 2, on_vector) if j == PLANES[-1][0] else (0, on_vector)
-            for first, end in zip(cuts, cuts[1:]):
-                nc.vector.tensor_copy(out=slot(j, first, end), in_=planes[j][:].indirect(entries(first, end)))
-            lead = keep.tile([P, S], BF16, name=f"lead{j}")
-            rest = keep.tile([P, S], BF16, name=f"rest{j}", tag=f"rest{min(j, 2)}")
+        lay = {"vector": nc.vector.tensor_copy, "gpsimd": nc.gpsimd.tensor_copy, "scalar": nc.scalar.copy}
+        for j, (direct, pieces) in enumerate(PLANES):
+            nc.vector.tensor_copy(out=slot(j, 0, direct), in_=picked(j, 0, direct))
+            staging = {}
+            for buffer, first, end, stretches in pieces:
+                if buffer not in staging:
+                    staging[buffer] = keep.tile([P, S], BF16, name=f"staged_{buffer}_{j}", tag=buffer, align_bytes=64)
+                nc.scalar.activation(out=staging[buffer][:, first:end], in_=picked(j, first, end), func=COPY)
+            for buffer, first, end, stretches in pieces:
+                for engine, start, stop in stretches:
+                    lay[engine](out=slot(j, start, stop), in_=staging[buffer][:, start:stop])
 
-            def staged(first, end):
-                return (lead if first == gathered[0][0] else rest)[:, first:end]
-
-            for first, end in gathered:
-                nc.scalar.activation(out=staged(first, end), in_=planes[j][:].indirect(entries(first, end)), func=COPY)
-            for first, end in by_gpsimd:
-                nc.gpsimd.tensor_copy(out=slot(j, first, end), in_=staged(first, end))
-            for first, end in by_scalar:
-                nc.scalar.copy(out=slot(j, first, end), in_=staged(first, end))
-
-        res_sb = keep.tile([P, U], F32, name="res_sb", tag=f"plane{PLANES[2][0]}")
+        res_sb = keep.tile([P, U], F32, name="res_sb", tag="plane2")
         for first, end in zip(RES_CUTS, RES_CUTS[1:]):
             nc.sync.dma_start(out=res_sb[:, first:end], in_=res[:, first:end])
 
+        head_codes = keep.tile([P, HEAD], U32, name="head_codes", tag="b3", align_bytes=64)
+        tail_codes = keep.tile([P, S - HEAD], U32, name="tail_codes", align_bytes=64)
+        scales = keep.tile([P, S], U8, name="scales", align_bytes=64)
         filled = []
-        for start, width, engines in BLOCKS:
-            codes = keep.tile([P, width], U32, name=f"codes{start}", align_bytes=64)
-            scales = keep.tile([P, width], U8, name=f"scales{start}", align_bytes=64)
-            nc.vector.quantize_mx(out=codes[:].bitcast(FP8X4), scales=scales[:], in_=woven[:, 4 * start : 4 * (start + width)])
-            part = width // len(engines)
-            for first, engine in zip(range(0, width, part), engines):
-                bank = psum.tile([P, part], F32, name=f"bank{start + first}")
+        for passes, engine in BANKS:
+            first, end = passes[0][0], sum(passes[-1])
+            bank = psum.tile([P, end - first], F32, name=f"bank{first}")
+            for start, width in passes:
+                codes = head_codes[:, start : start + width] if start < HEAD else tail_codes[:, start - HEAD : start - HEAD + width]
+                nc.vector.quantize_mx(out=codes.bitcast(FP8X4), scales=scales[:, start : start + width], in_=woven[:, 4 * start : 4 * (start + width)])
                 nc.tensor.matmul_mx(
-                    out=bank[:],
+                    out=bank[:, start - first : start - first + width],
                     lhsT=w_words[:].bitcast(FP8X4),
                     lhsT_scale=w_scales[:],
-                    rhs=codes[:, first : first + part].bitcast(FP8X4),
-                    rhs_scale=scales[:, first : first + part],
+                    rhs=codes.bitcast(FP8X4),
+                    rhs_scale=scales[:, start : start + width],
                     start=True,
                     stop=True,
                 )
-                filled.append((engine, start + first, start + first + part, bank))
+            filled.append((engine, first, end, bank))
         for engine, first, end, bank in filled:
             if engine == "vector":
                 nc.vector.tensor_scalar_max(out=y[:, first:end], in0=bank[:], scalar1=0.0)
             else:
                 nc.scalar.activation(out=y[:, first:end], in_=bank[:], func=RELU)
 
-        def owned(start, width):
-            return y[:].indirect(owners[:, start // LIST_ROWS : (start + width) // LIST_ROWS])
-
         start = 0
         for fetcher, width in OUT_PIECES:
             summed = keep.tile([P, width], F32, name=f"summed{start}")
-            addend = owned(start, width)
+            addend = y[:].indirect(owners[:, start // LIST_ROWS : (start + width) // LIST_ROWS])
             if fetcher == "scalar":
                 fetched = keep.tile([P, width], F32, name=f"fetched{start}")
                 nc.scalar.activation(out=fetched[:], in_=addend, func=COPY)

@@ -21,27 +21,24 @@ LIST_ROWS = 16
 PLANES = (
     (640, (("a0", 640, 768, (("gpsimd", 640, 768),)), ("b0", 768, 1024, (("gpsimd", 768, 1024),)))),
     (640, (("a1", 640, 768, (("gpsimd", 640, 768),)), ("b1", 768, 1024, (("gpsimd", 768, 1024),)))),
-    (512, (("a2", 832, 1024, (("gpsimd", 832, 1024),)), ("late", 640, 832, (("gpsimd", 640, 832),)), ("late", 512, 640, (("scalar", 512, 640),)))),
+    (512, (("a2", 640, 832, (("gpsimd", 640, 832),)), ("late", 832, 1024, (("gpsimd", 832, 1024),)), ("late", 512, 640, (("scalar", 512, 640),)))),
     (
-        448,
+        512,
         (
-            ("a3", 832, 896, (("gpsimd", 832, 896),)),
-            ("b3", 896, 1024, (("gpsimd", 896, 1024),)),
-            ("late", 448, 640, (("vector", 448, 512), ("scalar", 512, 640))),
-            ("late", 640, 832, (("scalar", 640, 768), ("scalar", 768, 832))),
+            ("b3", 640, 832, (("gpsimd", 640, 832),)),
+            ("late", 512, 640, (("scalar", 512, 640),)),
+            ("late", 832, 1024, (("scalar", 832, 960), ("scalar", 960, 1024))),
         ),
     ),
 )
 BANKS = (
-    (((832, 64),), "scalar"),
-    (((896, 128),), "scalar"),
-    (((0, 128), (128, 128)), "scalar"),
-    (((256, 128), (384, 128)), "vector"),
-    (((512, 128),), "scalar"),
-    (((640, 128),), "vector"),
-    (((768, 64),), "scalar"),
+    (((0, 64), (64, 128), (192, 128)), "scalar"),
+    (((320, 128),), "vector"),
+    (((704, 128),), "vector"),
+    (((448, 128), (576, 128)), "scalar"),
+    (((832, 128),), "vector"),
+    (((960, 64),), "scalar"),
 )
-HEAD = 512
 OUT_PIECES = (("vector", 384), ("scalar", 224), ("vector", 192), ("scalar", 320), ("vector", 192), ("scalar", 352), ("vector", 128), ("scalar", 256))
 RES_CUTS = (0, 384, 608, 1120, 1664, 2048)
 
@@ -79,7 +76,9 @@ def tile_picked_unmerge_relu_e_kernel(tc, xT, w1_words, w1_scales, res, offs, ow
 
         lay = {"vector": nc.vector.tensor_copy, "gpsimd": nc.gpsimd.tensor_copy, "scalar": nc.scalar.copy}
         for j, (direct, pieces) in enumerate(PLANES):
-            nc.vector.tensor_copy(out=slot(j, 0, direct), in_=picked(j, 0, direct))
+            cuts = (0, direct // 2, direct) if j == 3 else (0, direct)
+            for first, end in zip(cuts, cuts[1:]):
+                nc.vector.tensor_copy(out=slot(j, first, end), in_=picked(j, first, end))
             staging = {}
             for buffer, first, end, stretches in pieces:
                 if buffer not in staging:
@@ -93,15 +92,14 @@ def tile_picked_unmerge_relu_e_kernel(tc, xT, w1_words, w1_scales, res, offs, ow
         for first, end in zip(RES_CUTS, RES_CUTS[1:]):
             nc.sync.dma_start(out=res_sb[:, first:end], in_=res[:, first:end])
 
-        head_codes = keep.tile([P, HEAD], U32, name="head_codes", tag="b3", align_bytes=64)
-        tail_codes = keep.tile([P, S - HEAD], U32, name="tail_codes", align_bytes=64)
+        all_codes = keep.tile([P, S], U32, name="all_codes", align_bytes=64)
         scales = keep.tile([P, S], U8, name="scales", align_bytes=64)
         filled = []
         for passes, engine in BANKS:
             first, end = passes[0][0], sum(passes[-1])
             bank = psum.tile([P, end - first], F32, name=f"bank{first}")
             for start, width in passes:
-                codes = head_codes[:, start : start + width] if start < HEAD else tail_codes[:, start - HEAD : start - HEAD + width]
+                codes = all_codes[:, start : start + width]
                 nc.vector.quantize_mx(out=codes.bitcast(FP8X4), scales=scales[:, start : start + width], in_=woven[:, 4 * start : 4 * (start + width)])
                 nc.tensor.matmul_mx(
                     out=bank[:, start - first : start - first + width],

@@ -21,13 +21,13 @@ LIST_ROWS = 16
 PLANES = (
     (640, (("a0", 640, 768, (("gpsimd", 640, 768),)), ("b0", 768, 1024, (("gpsimd", 768, 1024),)))),
     (640, (("a1", 640, 768, (("gpsimd", 640, 768),)), ("b1", 768, 1024, (("gpsimd", 768, 1024),)))),
-    (512, (("a2", 640, 832, (("gpsimd", 640, 832),)), ("late", 832, 1024, (("gpsimd", 832, 1024),)), ("late", 512, 640, (("scalar", 512, 640),)))),
+    (512, (("a2", 640, 864, (("gpsimd", 640, 864),)), ("late", 864, 1024, (("gpsimd", 864, 1024),)), ("late", 512, 640, (("scalar", 512, 640),)))),
     (
         512,
         (
-            ("b3", 640, 832, (("gpsimd", 640, 832),)),
+            ("b3", 640, 864, (("gpsimd", 640, 864),)),
             ("late", 512, 640, (("scalar", 512, 640),)),
-            ("late", 832, 1024, (("scalar", 832, 960), ("scalar", 960, 1024))),
+            ("late", 864, 1024, (("scalar", 864, 960), ("scalar", 960, 1024))),
         ),
     ),
 )

@@ -32,13 +32,14 @@ PLANES = (
     ),
 )
 BANKS = (
-    (((0, 64), (64, 128), (192, 128)), "scalar"),
-    (((320, 128),), "vector"),
-    (((704, 128),), "vector"),
+    (((0, 64), (64, 128)), "scalar"),
+    (((704, 128),), "scalar"),
+    (((192, 128), (320, 128)), "vector"),
     (((448, 128), (576, 128)), "scalar"),
     (((832, 128),), "vector"),
     (((960, 64),), "scalar"),
 )
+HELD = (192, 448)
 OUT_PIECES = (("vector", 384), ("scalar", 224), ("vector", 192), ("scalar", 320), ("vector", 192), ("scalar", 352), ("vector", 128), ("scalar", 256))
 RES_CUTS = (0, 384, 608, 1120, 1664, 2048)
 
@@ -93,6 +94,7 @@ def tile_picked_unmerge_relu_e_kernel(tc, xT, w1_words, w1_scales, res, offs, ow
             nc.sync.dma_start(out=res_sb[:, first:end], in_=res[:, first:end])
 
         all_codes = keep.tile([P, S], U32, name="all_codes", align_bytes=64)
+        held_codes = keep.tile([P, HELD[1] - HELD[0]], U32, name="held_codes", tag="b3", align_bytes=64)
         scales = keep.tile([P, S], U8, name="scales", align_bytes=64)
         filled = []
         for passes, engine in BANKS:
@@ -100,6 +102,8 @@ def tile_picked_unmerge_relu_e_kernel(tc, xT, w1_words, w1_scales, res, offs, ow
             bank = psum.tile([P, end - first], F32, name=f"bank{first}")
             for start, width in passes:
                 codes = all_codes[:, start : start + width]
+                if HELD[0] <= start < HELD[1]:
+                    codes = held_codes[:, start - HELD[0] : start - HELD[0] + width]
                 nc.vector.quantize_mx(out=codes.bitcast(FP8X4), scales=scales[:, start : start + width], in_=woven[:, 4 * start : 4 * (start + width)])
                 nc.tensor.matmul_mx(
                     out=bank[:, start - first : start - first + width],

@@ -21,13 +21,13 @@ LIST_ROWS = 16
 PLANES = (
     (640, (("a0", 640, 768, (("gpsimd", 640, 768),)), ("b0", 768, 1024, (("gpsimd", 768, 1024),)))),
     (640, (("a1", 640, 768, (("gpsimd", 640, 768),)), ("b1", 768, 1024, (("gpsimd", 768, 1024),)))),
-    (512, (("a2", 640, 864, (("gpsimd", 640, 864),)), ("late", 864, 1024, (("gpsimd", 864, 1024),)), ("late", 512, 640, (("scalar", 512, 640),)))),
+    (512, (("a2", 640, 832, (("gpsimd", 640, 832),)), ("late", 832, 1024, (("gpsimd", 832, 1024),)), ("late", 512, 640, (("scalar", 512, 640),)))),
     (
         512,
         (
-            ("b3", 640, 864, (("gpsimd", 640, 864),)),
+            ("b3", 640, 832, (("gpsimd", 640, 832),)),
             ("late", 512, 640, (("scalar", 512, 640),)),
-            ("late", 864, 1024, (("scalar", 864, 960), ("scalar", 960, 1024))),
+            ("late", 832, 1024, (("scalar", 832, 960), ("scalar", 960, 1024))),
         ),
     ),
 )

@@ -26,20 +26,21 @@ PLANES = (
         512,
         (
             ("b3", 640, 832, (("gpsimd", 640, 832),)),
+            ("b3", 832, 896, (("scalar", 832, 896),)),
+            ("late", 896, 1024, (("scalar", 896, 1024),)),
             ("late", 512, 640, (("scalar", 512, 640),)),
-            ("late", 832, 1024, (("scalar", 832, 960), ("scalar", 960, 1024))),
         ),
     ),
 )
 BANKS = (
-    (((0, 64), (64, 128)), "scalar"),
-    (((704, 128),), "scalar"),
-    (((192, 128), (320, 128)), "vector"),
-    (((448, 128), (576, 128)), "scalar"),
-    (((832, 128),), "vector"),
-    (((960, 64),), "scalar"),
+    (((640, 128), (768, 128)), "scalar"),
+    (((0, 128), (128, 128)), "scalar"),
+    (((256, 128),), "scalar"),
+    (((384, 128),), "vector"),
+    (((896, 128),), "vector"),
+    (((512, 128),), "scalar"),
 )
-HELD = (192, 448)
+HELD = (0, 512)
 OUT_PIECES = (("vector", 384), ("scalar", 224), ("vector", 192), ("scalar", 320), ("vector", 192), ("scalar", 352), ("vector", 128), ("scalar", 256))
 RES_CUTS = (0, 384, 608, 1120, 1664, 2048)
 
@@ -77,9 +78,7 @@ def tile_picked_unmerge_relu_e_kernel(tc, xT, w1_words, w1_scales, res, offs, ow
 
         lay = {"vector": nc.vector.tensor_copy, "gpsimd": nc.gpsimd.tensor_copy, "scalar": nc.scalar.copy}
         for j, (direct, pieces) in enumerate(PLANES):
-            cuts = (0, direct // 2, direct) if j == 3 else (0, direct)
-            for first, end in zip(cuts, cuts[1:]):
-                nc.vector.tensor_copy(out=slot(j, first, end), in_=picked(j, first, end))
+            nc.vector.tensor_copy(out=slot(j, 0, direct), in_=picked(j, 0, direct))
             staging = {}
             for buffer, first, end, stretches in pieces:
                 if buffer not in staging:

@@ -25,20 +25,18 @@ PLANES = (
     (
         512,
         (
-            ("b3", 640, 832, (("gpsimd", 640, 832),)),
-            ("b3", 832, 896, (("scalar", 832, 896),)),
-            ("late", 896, 1024, (("scalar", 896, 1024),)),
-            ("late", 512, 640, (("scalar", 512, 640),)),
+            ("b3", 832, 1024, (("gpsimd", 832, 1024),)),
+            ("b3", 768, 832, (("scalar", 768, 832),)),
+            ("late", 512, 768, (("scalar", 512, 640), ("scalar", 640, 768))),
         ),
     ),
 )
 BANKS = (
-    (((640, 128), (768, 128)), "scalar"),
-    (((0, 128), (128, 128)), "scalar"),
-    (((256, 128),), "scalar"),
-    (((384, 128),), "vector"),
-    (((896, 128),), "vector"),
-    (((512, 128),), "scalar"),
+    (((896, 128), (768, 128)), "scalar"),
+    (((0, 128), (128, 128)), "vector"),
+    (((256, 128), (384, 128)), "scalar"),
+    (((512, 128),), "vector"),
+    (((640, 128),), "scalar"),
 )
 HELD = (0, 512)
 OUT_PIECES = (("vector", 384), ("scalar", 224), ("vector", 192), ("scalar", 320), ("vector", 192), ("scalar", 352), ("vector", 128), ("scalar", 256))
@@ -97,7 +95,7 @@ def tile_picked_unmerge_relu_e_kernel(tc, xT, w1_words, w1_scales, res, offs, ow
         scales = keep.tile([P, S], U8, name="scales", align_bytes=64)
         filled = []
         for passes, engine in BANKS:
-            first, end = passes[0][0], sum(passes[-1])
+            first, end = min(start for start, _ in passes), max(start + width for start, width in passes)
             bank = psum.tile([P, end - first], F32, name=f"bank{first}")
             for start, width in passes:
                 codes = all_codes[:, start : start + width]

from contextlib import ExitStack

import concourse.mybir as mybir

K, T, S, M, U = 512, 2048, 1024, 128, 2048
FLOPS = 2 * K * M * S

F32 = mybir.dt.float32
BF16 = mybir.dt.bfloat16
I32 = mybir.dt.int32
U32 = mybir.dt.uint32
U16 = mybir.dt.uint16
U8 = mybir.dt.uint8
FP8X4 = mybir.dt.float8_e4m3fn_x4
COPY = mybir.ActivationFunctionType.Copy
RELU = mybir.ActivationFunctionType.Relu
ADD = mybir.AluOpType.add

P = 128
LIST_ROWS = 16
PLANES = (
    (640, (("a0", 640, 768, (("gpsimd", 640, 768),)), ("b0", 768, 1024, (("gpsimd", 768, 1024),)))),
    (640, (("a1", 640, 768, (("gpsimd", 640, 768),)), ("b1", 768, 1024, (("gpsimd", 768, 1024),)))),
    (512, (("a2", 640, 832, (("gpsimd", 640, 832),)), ("late", 832, 1024, (("gpsimd", 832, 1024),)), ("late", 512, 640, (("scalar", 512, 640),)))),
    (
        512,
        (
            ("b3", 832, 1024, (("gpsimd", 832, 1024),)),
            ("b3", 768, 832, (("scalar", 768, 832),)),
            ("late", 512, 768, (("scalar", 512, 640), ("scalar", 640, 768))),
        ),
    ),
)
BANKS = (
    (((896, 128), (768, 128)), "scalar"),
    (((0, 128), (128, 128)), "vector"),
    (((256, 128), (384, 128)), "scalar"),
    (((512, 128),), "vector"),
    (((640, 128),), "scalar"),
)
HELD = (0, 512)
OUT_PIECES = (("vector", 384), ("scalar", 224), ("vector", 192), ("scalar", 320), ("vector", 192), ("scalar", 352), ("vector", 128), ("scalar", 256))
RES_CUTS = (0, 384, 608, 1120, 1664, 2048)


def tile_picked_unmerge_relu_e_kernel(tc, xT, w1_words, w1_scales, res, offs, own, out):
    nc = tc.nc
    rows = xT.rearrange("(p j) t -> p j t", j=4)
    with ExitStack() as ctx:
        keep = ctx.enter_context(tc.tile_pool(name="keep", bufs=1))
        psum = ctx.enter_context(tc.psum_pool(name="psum", bufs=1))

        picks = keep.tile([P, S // LIST_ROWS], U16, name="picks")
        owners = keep.tile([P, U // LIST_ROWS], U16, name="owners")
        w_words = keep.tile([P, M], U32, name="w_words", align_bytes=64)
        w_scales = keep.tile([P, M], U8, name="w_scales", align_bytes=64)
        y = keep.tile([P, S], F32, name="y")
        planes = [keep.tile([P, T], F32, name=f"plane{j}") for j in range(4)]
        woven = keep.tile([P, 4 * S], BF16, name="woven", align_bytes=64)

        nc.vector.memset(w_scales[:].bitcast(I32), 0)
        for j in range(4):
            nc.sync.dma_start(out=planes[j][:], in_=rows[:, j, :])
            if j == 0:
                nc.sync.dma_start(picks[:], offs)
        nc.sync.dma_start(out=w_words[:].bitcast(I32), in_=w1_words[0].rearrange("p n t -> p (n t)").bitcast(I32))
        for q in range(4):
            nc.sync.dma_start(out=w_scales[32 * q : 32 * q + 4, :].bitcast(I32), in_=w1_scales[0, 4 * q : 4 * q + 4, :].bitcast(I32))
        nc.sync.dma_start(owners[:], own)

        def slot(j, first, end):
            return woven[:, 4 * first : 4 * end].rearrange("p (n t) -> p n t", t=4)[:, :, j]

        def picked(j, first, end):
            return planes[j][:].indirect(picks[:, first // LIST_ROWS : end // LIST_ROWS])

        lay = {"vector": nc.vector.tensor_copy, "gpsimd": nc.gpsimd.tensor_copy, "scalar": nc.scalar.copy}
        for j, (direct, pieces) in enumerate(PLANES):
            nc.vector.tensor_copy(out=slot(j, 0, direct), in_=picked(j, 0, direct))
            staging = {}
            for buffer, first, end, stretches in pieces:
                if buffer not in staging:
                    staging[buffer] = keep.tile([P, S], BF16, name=f"staged_{buffer}_{j}", tag=buffer, align_bytes=64)
                nc.scalar.activation(out=staging[buffer][:, first:end], in_=picked(j, first, end), func=COPY)
            for buffer, first, end, stretches in pieces:
                for engine, start, stop in stretches:
                    lay[engine](out=slot(j, start, stop), in_=staging[buffer][:, start:stop])

        res_sb = keep.tile([P, U], F32, name="res_sb", tag="plane2")
        for first, end in zip(RES_CUTS, RES_CUTS[1:]):
            nc.sync.dma_start(out=res_sb[:, first:end], in_=res[:, first:end])

        all_codes = keep.tile([P, S], U32, name="all_codes", align_bytes=64)
        held_codes = keep.tile([P, HELD[1] - HELD[0]], U32, name="held_codes", tag="b3", align_bytes=64)
        scales = keep.tile([P, S], U8, name="scales", align_bytes=64)
        filled = []
        for passes, engine in BANKS:
            first, end = min(start for start, _ in passes), max(start + width for start, width in passes)
            bank = psum.tile([P, end - first], F32, name=f"bank{first}")
            for start, width in passes:
                codes = all_codes[:, start : start + width]
                if HELD[0] <= start < HELD[1]:
                    codes = held_codes[:, start - HELD[0] : start - HELD[0] + width]
                nc.vector.quantize_mx(out=codes.bitcast(FP8X4), scales=scales[:, start : start + width], in_=woven[:, 4 * start : 4 * (start + width)])
                nc.tensor.matmul_mx(
                    out=bank[:, start - first : start - first + width],
                    lhsT=w_words[:].bitcast(FP8X4),
                    lhsT_scale=w_scales[:],
                    rhs=codes.bitcast(FP8X4),
                    rhs_scale=scales[:, start : start + width],
                    start=True,
                    stop=True,
                )
            filled.append((engine, first, end, bank))
        for engine, first, end, bank in filled:
            if engine == "vector":
                nc.vector.tensor_scalar_max(out=y[:, first:end], in0=bank[:], scalar1=0.0)
            else:
                nc.scalar.activation(out=y[:, first:end], in_=bank[:], func=RELU)

        start = 0
        for fetcher, width in OUT_PIECES:
            summed = keep.tile([P, width], F32, name=f"summed{start}")
            addend = y[:].indirect(owners[:, start // LIST_ROWS : (start + width) // LIST_ROWS])
            if fetcher == "scalar":
                fetched = keep.tile([P, width], F32, name=f"fetched{start}")
                nc.scalar.activation(out=fetched[:], in_=addend, func=COPY)
                addend = fetched[:]
            nc.vector.tensor_tensor(out=summed[:], in0=addend, in1=res_sb[:, start : start + width], op=ADD)
            nc.sync.dma_start(out=out[:, start : start + width], in_=summed[:])
            start += width
